import numpy as np
import ml_dtypes


def mxq(x, axis, fmt="e4m3"):
    dtype, down = {"e4m3": (ml_dtypes.float8_e4m3fn, 7), "e5m2": (ml_dtypes.float8_e5m2, 14)}[fmt]
    v = np.moveaxis(np.asarray(x, np.float32).astype(ml_dtypes.bfloat16).astype(np.float64), axis, -1)
    blocks = v.reshape(v.shape[:-1] + (-1, 32))
    amax = np.abs(blocks).max(-1, keepdims=True)
    byte = np.maximum(np.where(amax > 0, np.frexp(amax)[1] - 1 + 127, 0) - down, 1)
    scale = np.exp2(byte - 127.0)
    codes = (blocks / scale).astype(np.float32).astype(dtype).astype(np.float64)
    return np.moveaxis((codes * scale).reshape(v.shape), -1, axis)


WIDE = False


def mx_kscale(k):
    if not WIDE:
        return np.ones(k)
    levels = np.array([10, -10, 5, -5, 0])
    if k % 512:
        return np.exp2(np.random.permutation(np.resize(levels, k // 32))).repeat(32)
    a = np.empty((k // 512, 16))
    for p in range(k // 512):
        a[p, :8] = np.random.permutation(np.resize(levels, 8))
        for g in range(8):
            far = levels[np.abs(levels - a[p, g]) >= 10]
            a[p, g + 8] = far[np.random.randint(len(far))]
    return np.exp2(a.ravel()).repeat(32)


def f64(x):
    return np.asarray(x).astype(np.float64)


def striped(idx):
    return np.tile(idx.reshape(-1, 16).T, (8, 1)).astype(np.uint16)


def unstriped(offs):
    return offs[:16].T.reshape(-1).astype(np.int64)


def striped8(idx):
    return np.concatenate([x.reshape(-1, 16).T for x in idx]).astype(np.uint16)


def runs(offs, k):
    lists = np.stack([offs[16 * r : 16 * r + 16].T.reshape(-1) for r in range(8)]).astype(np.int64)
    return lists[np.arange(k) % 512 // 64]


def pack_weight(w):
    k, n = w.shape
    w = f64(np.asarray(w, np.float32).astype(ml_dtypes.bfloat16)).reshape(k // 32, 32, n)
    amax = np.abs(w).max(1)
    byte = np.clip(np.where(amax > 0, np.frexp(amax)[1] - 1 + 127 - 7, 1), 1, 254)
    scaled = (w * np.exp2(127.0 - byte)[:, None, :]).reshape(k, n).astype(np.float32)
    words = np.ascontiguousarray(scaled.reshape(k // 512, 128, 4, n).transpose(0, 1, 3, 2)).astype(ml_dtypes.float8_e4m3fn).view(np.uint8)
    return words, np.ascontiguousarray(byte.astype(np.uint8).reshape(k // 512, 16, n))


def unpack_weight(words, scales):
    g, p, n, _ = words.shape
    vals = np.ascontiguousarray(words).view(ml_dtypes.float8_e4m3fn).astype(np.float64) * np.repeat(np.exp2(scales.astype(np.float64) - 127.0), 8, axis=1)[..., None]
    return vals.transpose(0, 1, 3, 2).reshape(g * 512, n)


def sigmoid(v):
    return 1.0 / (1.0 + np.exp(-np.maximum(v, -700.0)))


K, T, S, V, H = 512, 2048, 512, 256, 512


def setup_inputs():
    n = np.random.standard_normal
    s = mx_kscale(K)[:, None]
    u = mx_kscale(S)
    packed_xT = pack_weight(n((K, T)) * s)
    return {
        "x_words": packed_xT[0],
        "x_scales": packed_xT[1],
        "w1": (n((K, H)) / np.sqrt(K) / s).astype(np.float32),
        "w2": (n((K, H)) / np.sqrt(K) / s).astype(np.float32),
        "sl": np.random.uniform(1.0, 2.0, (H, 1)).astype(np.float32),
        "th": (0.5 * n((H, 1))).astype(np.float32),
        "ga": (np.random.uniform(0.5, 1.5, (H, 1)) * u[:, None]).astype(np.float32),
        "gb": (np.random.uniform(0.5, 1.5, (H, 1)) / u[:, None]).astype(np.float32),
        "tau": np.random.uniform(0.2, 0.6, (S, 1)).astype(np.float32),
        "tau2": np.random.uniform(0.6, 1.0, (S, 1)).astype(np.float32),
        "offs": striped(np.random.permutation(T)[:S]),
        "two": striped(np.random.permutation(T)[:V]),
        "n1": striped8(np.stack([np.random.permutation(S) for _ in range(8)])),
        "n2": striped8(np.stack([np.random.permutation(S) for _ in range(8)])),
        "n3": striped(np.random.permutation(V)),
        "n4": striped(np.random.permutation(V)),
        "n5": striped8(np.stack([np.random.permutation(V) for _ in range(8)])),
        "n6": striped8(np.stack([np.random.permutation(V) for _ in range(8)])),
    }


def reference(x_words, x_scales, w1, w2, sl, th, ga, gb, tau, tau2, offs, two, n1, n2, n3, n4, n5, n6):
    xq = unpack_weight(x_words, x_scales)[:, unstriped(offs)]
    a = mxq(f64(w1), 0, "e4m3").T @ xq
    sg = sigmoid(f64(sl) * (a[np.arange(H)[:, None], runs(n2, H)] - f64(th)))
    z = f64(ga) * (a + sg * (a[np.arange(H)[:, None], runs(n1, H)] - a))
    x_two = unpack_weight(x_words, x_scales)[:, unstriped(two)]
    b = mxq(f64(w2), 0, "e4m3").T @ x_two
    z2 = f64(gb) * (b[:, unstriped(n3)] * b[:, unstriped(n4)])
    s = 0.0625 * ((mxq(z, 0, "e4m3").T @ mxq(z2, 0, "e4m3")))
    top = s.max(axis=1, keepdims=True)
    ea = np.exp(f64(tau) * (s[np.arange(S)[:, None], runs(n5, S)] - top))
    ea2 = np.exp(f64(tau2) * (s[np.arange(S)[:, None], runs(n6, S)] - top))
    return 3.0 * (ea - ea2)

@@ -1,0 +1,213 @@
+from contextlib import ExitStack
+
+import concourse.mybir as mybir
+
+K, T, S, V, H = 512, 2048, 512, 256, 512
+FLOPS = 2 * K * H * S + 2 * K * H * V + 2 * H * S * V
+
+F32 = mybir.dt.float32
+BF16 = mybir.dt.bfloat16
+I32 = mybir.dt.int32
+U32 = mybir.dt.uint32
+U16 = mybir.dt.uint16
+U8 = mybir.dt.uint8
+FP8X4 = mybir.dt.float8_e4m3fn_x4
+ALU = mybir.AluOpType
+ACT = mybir.ActivationFunctionType
+
+P = 128
+PACK = 4
+SPARE_B = 16
+HALF = S // 2
+
+
+def tile_picked_kqetrprodetw_none_p_kernel(
+    tc, x_words, x_scales, w1, w2, sl, th, ga, gb, tau, tau2, offs, two, n1, n2, n3, n4, n5, n6, out
+):
+    nc = tc.nc
+    with ExitStack() as ctx:
+        lists = ctx.enter_context(tc.tile_pool(name="lists", bufs=1))
+        keep = ctx.enter_context(tc.tile_pool(name="keep", bufs=1))
+        psum = ctx.enter_context(tc.psum_pool(name="psum", bufs=1))
+
+        def load_list(name, src):
+            t = lists.tile([P, src.shape[1]], U16, name=name)
+            nc.sync.dma_start(t[:], src)
+            return t
+
+        def load_rows(name, src):
+            t = keep.tile([P, PACK], F32, name=name)
+            nc.gpsimd.dma_start(t[:], src.rearrange("(p t) o -> p (t o)", t=PACK))
+            return t
+
+        def load_weight(name, src):
+            t = keep.tile([P, PACK, H], F32, name=name, tag=name)
+            nc.sync.dma_start(t[:], src.rearrange("(p j) c -> p j c", j=PACK))
+            return t
+
+        scale_table = keep.tile([P, T], U8, name="scale_table")
+        nc.gpsimd.memset(scale_table[:].bitcast(I32), 0)
+        for q in range(4):
+            nc.scalar.dma_start(
+                scale_table[32 * q : 32 * q + 4, :].bitcast(I32), x_scales[0, 4 * q : 4 * q + 4, :].bitcast(I32)
+            )
+        two_l = load_list("two_l", two)
+        offs_l = load_list("offs_l", offs)
+        w2_raw = load_weight("w2_raw", w2)
+        n3_l = load_list("n3_l", n3)
+        n4_l = load_list("n4_l", n4)
+        word_table = keep.tile([P, T], I32, name="word_table")
+        nc.sync.dma_start(word_table[:], x_words[0].rearrange("p n t -> p (n t)").bitcast(I32))
+        n2_l = load_list("n2_l", n2)
+        n1_l = load_list("n1_l", n1)
+        w1_raw = load_weight("w1_raw", w1)
+        n5_l = load_list("n5_l", n5)
+        n6_l = load_list("n6_l", n6)
+
+        b_win = [keep.tile([P, V + SPARE_B], F32, name=f"b_win{t}") for t in range(PACK)]
+        s_win = [keep.tile([P, 2 * V], F32, name=f"s_win{u}") for u in range(PACK)]
+        for t in range(PACK):
+            nc.gpsimd.memset(b_win[t][:, V:], 0.0)
+        for u in range(PACK):
+            nc.gpsimd.memset(s_win[u][:, V:], 0.0)
+        sl_t = load_rows("sl_t", sl)
+        th_t = load_rows("th_t", th)
+        ga_t = load_rows("ga_t", ga)
+        gb_t = load_rows("gb_t", gb)
+        tau_t = load_rows("tau_t", tau)
+        tau2_t = load_rows("tau2_t", tau2)
+
+        neg_th = keep.tile([P, PACK], F32, name="neg_th")
+        sig_bias = keep.tile([P, PACK], F32, name="sig_bias")
+        nc.gpsimd.tensor_scalar(neg_th[:], th_t[:], -1.0, 0.0, ALU.mult, ALU.add)
+        nc.gpsimd.tensor_tensor(sig_bias[:], sl_t[:], neg_th[:], ALU.mult)
+        neg_tau = keep.tile([P, 2, PACK], F32, name="neg_tau")
+        nc.gpsimd.tensor_scalar(neg_tau[:, 0, :], tau_t[:], -1.0, 0.0, ALU.mult, ALU.add)
+        nc.gpsimd.tensor_scalar(neg_tau[:, 1, :], tau2_t[:], -1.0, 0.0, ALU.mult, ALU.add)
+
+        def pick_scales(name, offsets, n):
+            scales = keep.tile([P, n], U8, name=name, align_bytes=64)
+            nc.vector.tensor_copy(scales[:], scale_table[:].indirect(offsets[:]))
+            return scales
+
+        def pick_words(name, offsets, n):
+            words = keep.tile([P, n], U32, name=name, align_bytes=64)
+            nc.vector.tensor_copy(words[:], word_table[:].bitcast(U32).indirect(offsets[:]))
+            return words
+
+        def quantise(name, grouped, n):
+            codes = keep.tile([P, n], U32, name=name + "_codes", align_bytes=64)
+            scales = keep.tile([P, n], U8, name=name + "_scales", align_bytes=64)
+            nc.vector.quantize_mx(out=codes[:].bitcast(FP8X4), scales=scales[:], in_=grouped)
+            return codes, scales
+
+        def weight_pair(name, raw, pair, copy):
+            grouped = keep.tile([P, 2, PACK * P], BF16, name=name + "_bf", align_bytes=64)
+            copy(
+                grouped[:].rearrange("p t (m j) -> p m j t", j=PACK),
+                raw[:].rearrange("p j (m a t) -> p a m j t", a=2, t=2)[:, pair],
+            )
+            return quantise(name, grouped[:].rearrange("p t c -> p (t c)"), 2 * P)
+
+        def product(tag, n, lhs, slot, rhs):
+            acc = psum.tile([P, n], F32, tag=tag, name=tag)
+            cols = slice(slot * P, (slot + 1) * P)
+            nc.tensor.matmul_mx(
+                out=acc[:],
+                lhsT=lhs[0][:, cols].bitcast(FP8X4),
+                lhsT_scale=lhs[1][:, cols],
+                rhs=rhs[0][:].bitcast(FP8X4),
+                rhs_scale=rhs[1][:],
+                start=True,
+                stop=True,
+            )
+            return acc
+
+        xb_scales = pick_scales("xb_scales", two_l, V)
+        w2_q = [
+            weight_pair("w2a", w2_raw, 0, nc.scalar.copy),
+            weight_pair("w2b", w2_raw, 1, nc.scalar.copy),
+        ]
+        xb_words = pick_words("xb_words", two_l, V)
+        xa_scales = pick_scales("xa_scales", offs_l, S)
+        xa_words = pick_words("xa_words", offs_l, S)
+        w1_q = [
+            weight_pair("w1a", w1_raw, 0, nc.vector.tensor_copy),
+            weight_pair("w1b", w1_raw, 1, nc.vector.tensor_copy),
+        ]
+        b_prod = keep.tile([P, PACK, V], F32, name="b_prod", tag="w1_raw")
+        for t in range(PACK):
+            acc = product(f"narrow{t}", V, w2_q[t // 2], t % 2, (xb_words, xb_scales))
+            nc.scalar.copy(b_win[t][:, :V], acc[:])
+            b3 = keep.tile([P, V], F32, name=f"b3_{t}")
+            nc.scalar.activation(b3[:], b_win[t][:].indirect(n3_l[:]), ACT.Copy)
+            nc.vector.tensor_tensor(b_prod[:, t, :], b_win[t][:].indirect(n4_l[:]), b3[:], ALU.mult)
+
+        z2_bf = keep.tile([P, V, PACK], BF16, name="z2_bf", align_bytes=64)
+        nc.vector.tensor_tensor(
+            z2_bf[:].rearrange("p (c i) t -> p c t i", i=4),
+            b_prod[:].rearrange("p t (c i) -> p c t i", i=4),
+            gb_t[:].rearrange("p (c t i) -> p c t i", c=1, i=1).to_broadcast([P, V // 4, PACK, 4]),
+            ALU.mult,
+        )
+        z2_q = quantise("z2", z2_bf[:].rearrange("p v t -> p (v t)"), V)
+
+        far = keep.tile([P, PACK, S], F32, name="far")
+        near = keep.tile([P, PACK, S], F32, name="near")
+        for t in range(PACK):
+            acc = product(f"wide{t}", S, w1_q[t // 2], t % 2, (xa_words, xa_scales))
+            a_win = keep.tile([P, S], F32, name=f"a_win{t}")
+            ga_win = keep.tile([P, S], F32, name=f"ga_win{t}")
+            sg = keep.tile([P, S], F32, name=f"sg{t}")
+            nc.scalar.copy(a_win[:], acc[:])
+            nc.scalar.activation(ga_win[:], acc[:], ACT.Copy, scale=ga_t[:, t : t + 1])
+            for h in range(2):
+                cols = slice(h * HALF, (h + 1) * HALF)
+                entries = slice(h * HALF // 16, (h + 1) * HALF // 16)
+                nc.scalar.activation(
+                    sg[:, cols],
+                    a_win[:].indirect(n2_l[:, entries]),
+                    ACT.Sigmoid,
+                    bias=sig_bias[:, t : t + 1],
+                    scale=sl_t[:, t : t + 1],
+                )
+                nc.vector.tensor_tensor(far[:, t, cols], ga_win[:].indirect(n1_l[:, entries]), sg[:, cols], ALU.mult)
+                nc.vector.scalar_tensor_tensor(
+                    near[:, t, cols], sg[:, cols], 1.0, ga_win[:, cols], ALU.subtract, ALU.mult
+                )
+
+        out_rows = out.rearrange("(p u) v -> p u v", u=PACK)
+        exp_bias = []
+        for pair in range(2):
+            z_bf = keep.tile([P, 2, PACK * P], BF16, name=f"z_bf{pair}", align_bytes=64)
+            for h in range(2):
+                places = slice(h * P // 2, (h + 1) * P // 2)
+                nc.vector.tensor_tensor(
+                    z_bf[:].rearrange("p u (m t) -> p m t u", t=PACK)[:, places],
+                    far[:].rearrange("p t (m a u) -> p a m t u", a=2, u=2)[:, pair, places],
+                    near[:].rearrange("p t (m a u) -> p a m t u", a=2, u=2)[:, pair, places],
+                    ALU.subtract,
+                )
+            z_q = quantise(f"z{pair}", z_bf[:].rearrange("p u c -> p (u c)"), 2 * P)
+            for slot in range(2):
+                u = 2 * pair + slot
+                acc = product(f"narrow{u}", V, z_q, slot, z2_q)
+                top = keep.tile([P, 1], F32, name=f"top{u}")
+                nc.vector.tensor_scalar(s_win[u][:, :V], acc[:], 0.0625, None, ALU.mult, ALU.max, accum_out=top[:])
+                bias = keep.tile([P, 2], F32, name=f"exp_bias{u}")
+                nc.vector.tensor_scalar(bias[:], neg_tau[:, :, u], top[:], None, ALU.mult)
+                exp_bias.append(bias)
+        for u in range(PACK):
+            ea = keep.tile([P, V], F32, name=f"ea{u}")
+            ea2 = keep.tile([P, V], F32, name=f"ea2_{u}")
+            nc.scalar.activation(
+                ea2[:], s_win[u][:].indirect(n6_l[:]), ACT.Exp, bias=exp_bias[u][:, 1:2], scale=tau2_t[:, u : u + 1]
+            )
+            nc.scalar.activation(
+                ea[:], s_win[u][:].indirect(n5_l[:]), ACT.Exp, bias=exp_bias[u][:, 0:1], scale=tau_t[:, u : u + 1]
+            )
+            ea2_3 = keep.tile([P, V], F32, name=f"ea2_3_{u}")
+            nc.vector.tensor_scalar(ea2_3[:], ea2[:], 3.0, None, ALU.mult)
+            result = keep.tile([P, V], F32, name=f"result{u}")
+            nc.vector.scalar_tensor_tensor(result[:], ea[:], 3.0, ea2_3[:], ALU.mult, ALU.subtract)
+            nc.sync.dma_start(out_rows[:, u, :], result[:])

@@ -66,10 +66,6 @@ def tile_picked_kqetrprodetw_none_p_kernel(
 
         b_win = [keep.tile([P, V + SPARE_B], F32, name=f"b_win{t}") for t in range(PACK)]
         s_win = [keep.tile([P, 2 * V], F32, name=f"s_win{u}") for u in range(PACK)]
-        for t in range(PACK):
-            nc.gpsimd.memset(b_win[t][:, V:], 0.0)
-        for u in range(PACK):
-            nc.gpsimd.memset(s_win[u][:, V:], 0.0)
         sl_t = load_rows("sl_t", sl)
         th_t = load_rows("th_t", th)
         ga_t = load_rows("ga_t", ga)
@@ -156,14 +152,15 @@ def tile_picked_kqetrprodetw_none_p_kernel(
         near = keep.tile([P, PACK, S], F32, name="near")
         for t in range(PACK):
             acc = product(f"wide{t}", S, w1_q[t // 2], t % 2, (xa_words, xa_scales))
-            a_win = keep.tile([P, S], F32, name=f"a_win{t}")
-            ga_win = keep.tile([P, S], F32, name=f"ga_win{t}")
+            a_win = keep.tile([P, 2 * S], F32, name=f"a_win{t}")
+            ga_win = keep.tile([P, 2 * S], F32, name=f"ga_win{t}")
+            nc.scalar.copy(a_win[:, :S], acc[:])
+            nc.scalar.activation(ga_win[:, :S], acc[:], ACT.Copy, scale=ga_t[:, t : t + 1])
             sg = keep.tile([P, S], F32, name=f"sg{t}")
-            nc.scalar.copy(a_win[:], acc[:])
-            nc.scalar.activation(ga_win[:], acc[:], ACT.Copy, scale=ga_t[:, t : t + 1])
-            for h in range(2):
-                cols = slice(h * HALF, (h + 1) * HALF)
-                entries = slice(h * HALF // 16, (h + 1) * HALF // 16)
+            width = HALF if t == PACK - 1 else S
+            for start in range(0, S, width):
+                cols = slice(start, start + width)
+                entries = slice(start // 16, (start + width) // 16)
                 nc.scalar.activation(
                     sg[:, cols],
                     a_win[:].indirect(n2_l[:, entries]),
@@ -179,7 +176,7 @@ def tile_picked_kqetrprodetw_none_p_kernel(
         out_rows = out.rearrange("(p u) v -> p u v", u=PACK)
         exp_bias = []
         for pair in range(2):
-            z_bf = keep.tile([P, 2, PACK * P], BF16, name=f"z_bf{pair}", align_bytes=64)
+            z_bf = keep.tile([P, 2, PACK * P], BF16, name=f"z_bf{pair}", tag="z_bf", align_bytes=64)
             for h in range(2):
                 places = slice(h * P // 2, (h + 1) * P // 2)
                 nc.vector.tensor_tensor(

from contextlib import ExitStack

import concourse.mybir as mybir

K, T, S, V, H = 512, 2048, 512, 256, 512
FLOPS = 2 * K * H * S + 2 * K * H * V + 2 * H * S * V

F32 = mybir.dt.float32
BF16 = mybir.dt.bfloat16
I32 = mybir.dt.int32
U32 = mybir.dt.uint32
U16 = mybir.dt.uint16
U8 = mybir.dt.uint8
FP8X4 = mybir.dt.float8_e4m3fn_x4
ALU = mybir.AluOpType
ACT = mybir.ActivationFunctionType

P = 128
PACK = 4
SPARE_B = 16
HALF = S // 2


def tile_picked_kqetrprodetw_none_p_kernel(
    tc, x_words, x_scales, w1, w2, sl, th, ga, gb, tau, tau2, offs, two, n1, n2, n3, n4, n5, n6, out
):
    nc = tc.nc
    with ExitStack() as ctx:
        lists = ctx.enter_context(tc.tile_pool(name="lists", bufs=1))
        keep = ctx.enter_context(tc.tile_pool(name="keep", bufs=1))
        psum = ctx.enter_context(tc.psum_pool(name="psum", bufs=1))

        def load_list(name, src):
            t = lists.tile([P, src.shape[1]], U16, name=name)
            nc.sync.dma_start(t[:], src)
            return t

        def load_rows(name, src):
            t = keep.tile([P, PACK], F32, name=name)
            nc.gpsimd.dma_start(t[:], src.rearrange("(p t) o -> p (t o)", t=PACK))
            return t

        def load_weight(name, src):
            t = keep.tile([P, PACK, H], F32, name=name, tag=name)
            nc.sync.dma_start(t[:], src.rearrange("(p j) c -> p j c", j=PACK))
            return t

        scale_table = keep.tile([P, T], U8, name="scale_table")
        nc.gpsimd.memset(scale_table[:].bitcast(I32), 0)
        for q in range(4):
            nc.scalar.dma_start(
                scale_table[32 * q : 32 * q + 4, :].bitcast(I32), x_scales[0, 4 * q : 4 * q + 4, :].bitcast(I32)
            )
        two_l = load_list("two_l", two)
        offs_l = load_list("offs_l", offs)
        w2_raw = load_weight("w2_raw", w2)
        n3_l = load_list("n3_l", n3)
        n4_l = load_list("n4_l", n4)
        word_table = keep.tile([P, T], I32, name="word_table")
        nc.sync.dma_start(word_table[:], x_words[0].rearrange("p n t -> p (n t)").bitcast(I32))
        n2_l = load_list("n2_l", n2)
        n1_l = load_list("n1_l", n1)
        w1_raw = load_weight("w1_raw", w1)
        n5_l = load_list("n5_l", n5)
        n6_l = load_list("n6_l", n6)

        b_win = [keep.tile([P, V + SPARE_B], F32, name=f"b_win{t}") for t in range(PACK)]
        s_win = [keep.tile([P, 2 * V], F32, name=f"s_win{u}") for u in range(PACK)]
        sl_t = load_rows("sl_t", sl)
        th_t = load_rows("th_t", th)
        ga_t = load_rows("ga_t", ga)
        gb_t = load_rows("gb_t", gb)
        tau_t = load_rows("tau_t", tau)
        tau2_t = load_rows("tau2_t", tau2)

        neg_th = keep.tile([P, PACK], F32, name="neg_th")
        sig_bias = keep.tile([P, PACK], F32, name="sig_bias")
        nc.gpsimd.tensor_scalar(neg_th[:], th_t[:], -1.0, 0.0, ALU.mult, ALU.add)
        nc.gpsimd.tensor_tensor(sig_bias[:], sl_t[:], neg_th[:], ALU.mult)
        neg_tau = keep.tile([P, 2, PACK], F32, name="neg_tau")
        nc.gpsimd.tensor_scalar(neg_tau[:, 0, :], tau_t[:], -1.0, 0.0, ALU.mult, ALU.add)
        nc.gpsimd.tensor_scalar(neg_tau[:, 1, :], tau2_t[:], -1.0, 0.0, ALU.mult, ALU.add)

        def pick_scales(name, offsets, n):
            scales = keep.tile([P, n], U8, name=name, align_bytes=64)
            nc.vector.tensor_copy(scales[:], scale_table[:].indirect(offsets[:]))
            return scales

        def pick_words(name, offsets, n):
            words = keep.tile([P, n], U32, name=name, align_bytes=64)
            nc.vector.tensor_copy(words[:], word_table[:].bitcast(U32).indirect(offsets[:]))
            return words

        def quantise(name, grouped, n):
            codes = keep.tile([P, n], U32, name=name + "_codes", align_bytes=64)
            scales = keep.tile([P, n], U8, name=name + "_scales", align_bytes=64)
            nc.vector.quantize_mx(out=codes[:].bitcast(FP8X4), scales=scales[:], in_=grouped)
            return codes, scales

        def weight_pair(name, raw, pair, copy):
            grouped = keep.tile([P, 2, PACK * P], BF16, name=name + "_bf", align_bytes=64)
            copy(
                grouped[:].rearrange("p t (m j) -> p m j t", j=PACK),
                raw[:].rearrange("p j (m a t) -> p a m j t", a=2, t=2)[:, pair],
            )
            return quantise(name, grouped[:].rearrange("p t c -> p (t c)"), 2 * P)

        def product(tag, n, lhs, slot, rhs):
            acc = psum.tile([P, n], F32, tag=tag, name=tag)
            cols = slice(slot * P, (slot + 1) * P)
            nc.tensor.matmul_mx(
                out=acc[:],
                lhsT=lhs[0][:, cols].bitcast(FP8X4),
                lhsT_scale=lhs[1][:, cols],
                rhs=rhs[0][:].bitcast(FP8X4),
                rhs_scale=rhs[1][:],
                start=True,
                stop=True,
            )
            return acc

        xb_scales = pick_scales("xb_scales", two_l, V)
        w2_q = [
            weight_pair("w2a", w2_raw, 0, nc.scalar.copy),
            weight_pair("w2b", w2_raw, 1, nc.scalar.copy),
        ]
        xb_words = pick_words("xb_words", two_l, V)
        xa_scales = pick_scales("xa_scales", offs_l, S)
        xa_words = pick_words("xa_words", offs_l, S)
        w1_q = [
            weight_pair("w1a", w1_raw, 0, nc.vector.tensor_copy),
            weight_pair("w1b", w1_raw, 1, nc.vector.tensor_copy),
        ]
        b_prod = keep.tile([P, PACK, V], F32, name="b_prod", tag="w1_raw")
        for t in range(PACK):
            acc = product(f"narrow{t}", V, w2_q[t // 2], t % 2, (xb_words, xb_scales))
            nc.scalar.copy(b_win[t][:, :V], acc[:])
            b3 = keep.tile([P, V], F32, name=f"b3_{t}")
            nc.scalar.activation(b3[:], b_win[t][:].indirect(n3_l[:]), ACT.Copy)
            nc.vector.tensor_tensor(b_prod[:, t, :], b_win[t][:].indirect(n4_l[:]), b3[:], ALU.mult)

        z2_bf = keep.tile([P, V, PACK], BF16, name="z2_bf", align_bytes=64)
        nc.vector.tensor_tensor(
            z2_bf[:].rearrange("p (c i) t -> p c t i", i=4),
            b_prod[:].rearrange("p t (c i) -> p c t i", i=4),
            gb_t[:].rearrange("p (c t i) -> p c t i", c=1, i=1).to_broadcast([P, V // 4, PACK, 4]),
            ALU.mult,
        )
        z2_q = quantise("z2", z2_bf[:].rearrange("p v t -> p (v t)"), V)

        far = keep.tile([P, PACK, S], F32, name="far")
        near = keep.tile([P, PACK, S], F32, name="near")
        for t in range(PACK):
            acc = product(f"wide{t}", S, w1_q[t // 2], t % 2, (xa_words, xa_scales))
            a_win = keep.tile([P, 2 * S], F32, name=f"a_win{t}")
            ga_win = keep.tile([P, 2 * S], F32, name=f"ga_win{t}")
            nc.scalar.copy(a_win[:, :S], acc[:])
            nc.scalar.activation(ga_win[:, :S], acc[:], ACT.Copy, scale=ga_t[:, t : t + 1])
            sg = keep.tile([P, S], F32, name=f"sg{t}")
            width = HALF if t == PACK - 1 else S
            for start in range(0, S, width):
                cols = slice(start, start + width)
                entries = slice(start // 16, (start + width) // 16)
                nc.scalar.activation(
                    sg[:, cols],
                    a_win[:].indirect(n2_l[:, entries]),
                    ACT.Sigmoid,
                    bias=sig_bias[:, t : t + 1],
                    scale=sl_t[:, t : t + 1],
                )
                nc.vector.tensor_tensor(far[:, t, cols], ga_win[:].indirect(n1_l[:, entries]), sg[:, cols], ALU.mult)
                nc.vector.scalar_tensor_tensor(
                    near[:, t, cols], sg[:, cols], 1.0, ga_win[:, cols], ALU.subtract, ALU.mult
                )

        out_rows = out.rearrange("(p u) v -> p u v", u=PACK)
        exp_bias = []
        for pair in range(2):
            z_bf = keep.tile([P, 2, PACK * P], BF16, name=f"z_bf{pair}", tag="z_bf", align_bytes=64)
            for h in range(2):
                places = slice(h * P // 2, (h + 1) * P // 2)
                nc.vector.tensor_tensor(
                    z_bf[:].rearrange("p u (m t) -> p m t u", t=PACK)[:, places],
                    far[:].rearrange("p t (m a u) -> p a m t u", a=2, u=2)[:, pair, places],
                    near[:].rearrange("p t (m a u) -> p a m t u", a=2, u=2)[:, pair, places],
                    ALU.subtract,
                )
            z_q = quantise(f"z{pair}", z_bf[:].rearrange("p u c -> p (u c)"), 2 * P)
            for slot in range(2):
                u = 2 * pair + slot
                acc = product(f"narrow{u}", V, z_q, slot, z2_q)
                top = keep.tile([P, 1], F32, name=f"top{u}")
                nc.vector.tensor_scalar(s_win[u][:, :V], acc[:], 0.0625, None, ALU.mult, ALU.max, accum_out=top[:])
                bias = keep.tile([P, 2], F32, name=f"exp_bias{u}")
                nc.vector.tensor_scalar(bias[:], neg_tau[:, :, u], top[:], None, ALU.mult)
                exp_bias.append(bias)
        for u in range(PACK):
            ea = keep.tile([P, V], F32, name=f"ea{u}")
            ea2 = keep.tile([P, V], F32, name=f"ea2_{u}")
            nc.scalar.activation(
                ea2[:], s_win[u][:].indirect(n6_l[:]), ACT.Exp, bias=exp_bias[u][:, 1:2], scale=tau2_t[:, u : u + 1]
            )
            nc.scalar.activation(
                ea[:], s_win[u][:].indirect(n5_l[:]), ACT.Exp, bias=exp_bias[u][:, 0:1], scale=tau_t[:, u : u + 1]
            )
            ea2_3 = keep.tile([P, V], F32, name=f"ea2_3_{u}")
            nc.vector.tensor_scalar(ea2_3[:], ea2[:], 3.0, None, ALU.mult)
            result = keep.tile([P, V], F32, name=f"result{u}")
            nc.vector.scalar_tensor_tensor(result[:], ea[:], 3.0, ea2_3[:], ALU.mult, ALU.subtract)
            nc.sync.dma_start(out_rows[:, u, :], result[:])
